import numpy as np
import ml_dtypes


def mxq(x, axis, fmt="e4m3"):
    dtype, down = {"e4m3": (ml_dtypes.float8_e4m3fn, 7), "e5m2": (ml_dtypes.float8_e5m2, 14)}[fmt]
    v = np.moveaxis(np.asarray(x, np.float32).astype(ml_dtypes.bfloat16).astype(np.float64), axis, -1)
    blocks = v.reshape(v.shape[:-1] + (-1, 32))
    amax = np.abs(blocks).max(-1, keepdims=True)
    byte = np.maximum(np.where(amax > 0, np.frexp(amax)[1] - 1 + 127, 0) - down, 1)
    scale = np.exp2(byte - 127.0)
    codes = (blocks / scale).astype(np.float32).astype(dtype).astype(np.float64)
    return np.moveaxis((codes * scale).reshape(v.shape), -1, axis)


WIDE = False


def mx_kscale(k):
    if not WIDE:
        return np.ones(k)
    levels = np.array([10, -10, 5, -5, 0])
    if k % 512:
        return np.exp2(np.random.permutation(np.resize(levels, k // 32))).repeat(32)
    a = np.empty((k // 512, 16))
    for p in range(k // 512):
        a[p, :8] = np.random.permutation(np.resize(levels, 8))
        for g in range(8):
            far = levels[np.abs(levels - a[p, g]) >= 10]
            a[p, g + 8] = far[np.random.randint(len(far))]
    return np.exp2(a.ravel()).repeat(32)


def f64(x):
    return np.asarray(x).astype(np.float64)


def striped(idx):
    return np.tile(np.asarray(idx).reshape(-1, 16).T, (8, 1)).astype(np.uint16)


def unstriped(offs):
    return offs[:16].T.reshape(-1).astype(np.int64)


E2M1 = np.array([0.0, 0.5, 1.0, 1.5, 2.0, 3.0, 4.0, 6.0, -0.0, -0.5, -1.0, -1.5, -2.0, -3.0, -4.0, -6.0])


def pack_weight(w, fmt):
    k, n = w.shape
    w = f64(np.asarray(w, np.float32).astype(ml_dtypes.bfloat16)).reshape(k // 32, 32, n)
    amax = np.abs(w).max(1)
    if fmt == "e4m3":
        byte = np.frexp(amax)[1] - 1 + 127 - 7
    else:
        mant, ex = np.frexp(amax / 6.0)
        byte = np.where(mant > 0.5, ex, ex - 1) + 127
    byte = np.clip(np.where(amax > 0, byte, 1), 1, 254)
    scaled = (w * np.exp2(127.0 - byte)[:, None, :]).reshape(k, n).astype(np.float32)
    by_word = np.ascontiguousarray(scaled.reshape(k // 512, 128, 4, n).transpose(0, 1, 3, 2))
    if fmt == "e4m3":
        words = by_word.astype(ml_dtypes.float8_e4m3fn).view(np.uint8)
    else:
        c = by_word.astype(ml_dtypes.float4_e2m1fn).view(np.uint8) & 0xF
        words = (c[..., 0::2] | (c[..., 1::2] << 4)).reshape(k // 512, 128, 2 * n)
    return np.ascontiguousarray(words), np.ascontiguousarray(byte.astype(np.uint8).reshape(k // 512, 16, n))


def unpack_weight(words, scales, fmt):
    g, _, n = scales.shape
    words = np.ascontiguousarray(words).reshape(g, 128, n, -1)
    if fmt == "e4m3":
        vals = words.view(ml_dtypes.float8_e4m3fn).astype(np.float64)
    else:
        nib = np.empty((g, 128, n, 4), np.uint8)
        nib[..., 0::2] = words & 0xF
        nib[..., 1::2] = words >> 4
        vals = E2M1[nib]
    vals = vals * np.repeat(np.exp2(scales.astype(np.float64) - 127.0), 8, axis=1)[..., None]
    return vals.transpose(0, 1, 3, 2).reshape(g * 512, n)


D, K, R, T, I, Q, G = 512, 512, 512, 2048, 512, 128, 64


def setup_inputs():
    n = np.random.standard_normal
    idx = np.random.permutation(T)[:I]
    fd = mx_kscale(D)
    fk = mx_kscale(K)
    fi = mx_kscale(I)
    keysp = pack_weight(n((D, T)) / fd[:, None], "e2m1")
    tabp = pack_weight(n((K, T)) / fk[:, None], "e2m1")
    return {
        "query": (n((D, Q)) * 0.7 / np.sqrt(D) * fd[:, None]).astype(np.float32),
        "keys_words": keysp[0],
        "keys_scales": keysp[1],
        "tab_words": tabp[0],
        "tab_scales": tabp[1],
        "w1": (n((K, R)) * 1 / np.sqrt(K) * fk[:, None]).astype(np.float32),
        "temper": (np.random.uniform(0.4, 1.0, (R, 1))).astype(np.float32),
        "os": (np.random.uniform(4.0, 16.0, (1, I)) * fi).astype(np.float32),
        "vs": (np.random.uniform(0.5, 2.0, (1, I)) / fi).astype(np.float32),
        "offs": striped(idx),
    }


def reference(query, keys_words, keys_scales, tab_words, tab_scales, w1, temper, os, vs, offs):
    idx = unstriped(offs)
    keysu = unpack_weight(keys_words, keys_scales, "e2m1")
    tabu = unpack_weight(tab_words, tab_scales, "e2m1")
    queryq = mxq(f64(query), 0, "e4m3")
    keysidxg = keysu[:, idx]
    a = queryq.T @ keysidxg
    p = np.exp(a - np.max(a, axis=1, keepdims=True))
    z = np.sum(p, axis=1, keepdims=True)
    w = p / z
    w1q = mxq(f64(w1), 0, "e4m3")
    tabidxg = tabu[:, idx]
    zh = w1q.T @ tabidxg
    ht = np.exp(zh * f64(temper))
    mz = ht.reshape(R, G, I // G).sum(axis=2)
    mzr = np.repeat(mz, I // G, axis=1)
    hv = ht / mzr * 4.0
    wo1 = w * f64(os)
    wt1 = wo1.T
    hw = hv * f64(vs)
    ht1 = hw.T
    wt1q = mxq(wt1, 0, "e4m3")
    ht1q = mxq(ht1, 0, "e4m3")
    o = wt1q.T @ ht1q
    return o

@@ -1,0 +1,223 @@
+from contextlib import ExitStack
+
+import concourse.mybir as mybir
+from concourse.masks import make_identity
+
+F32 = mybir.dt.float32
+BF16 = mybir.dt.bfloat16
+I32 = mybir.dt.int32
+U32 = mybir.dt.uint32
+U16 = mybir.dt.uint16
+U8 = mybir.dt.uint8
+FP8X4 = mybir.dt.float8_e4m3fn_x4
+FP4X4 = mybir.dt.float4_e2m1fn_x4
+ACT = mybir.ActivationFunctionType
+ALU = mybir.AluOpType
+AXIS = mybir.AxisListType
+
+P = 128
+PACK = 4
+POOL = 2048
+SLOTS = 512
+HIDDEN = 512
+TILES = HIDDEN // P
+GROUPS = SLOTS // 8
+RUN = 4
+
+FLOPS = 2 * 128 * 512 * 512 + 2 * 512 * 512 * 512 + 2 * 128 * 512 * 512
+
+
+def tile_attend_lrshared_soft_kernel(tc, query, keys_words, keys_scales, tab_words, tab_scales, w1, temper, slot_factor, slot_scale, offs, out):
+    nc = tc.nc
+    with ExitStack() as ctx:
+        keep = ctx.enter_context(tc.tile_pool(name="keep", bufs=1))
+        psum = ctx.enter_context(tc.psum_pool(name="psum", bufs=2))
+
+        def sbuf(name, shape, dtype):
+            return keep.tile(shape, dtype, name=name, align_bytes=64)
+
+        def load_scale_rows(window, scales):
+            nc.vector.memset(window[:].bitcast(I32), 0)
+            for quadrant in range(4):
+                nc.sync.dma_start(
+                    out=window[32 * quadrant : 32 * quadrant + 4, :].bitcast(I32),
+                    in_=scales[0, 4 * quadrant : 4 * quadrant + 4, :].bitcast(I32),
+                )
+
+        def gather(name, window, dtype):
+            listed = sbuf(name, [P, SLOTS], dtype)
+            nc.vector.tensor_copy(listed[:], window[:].indirect(offsets[:]))
+            return listed
+
+        def round_and_weave(name, planes):
+            woven = sbuf(name, [P, P, PACK], BF16)
+            nc.scalar.copy(
+                out=woven[:].rearrange("p (c i) t -> p c t i", i=RUN),
+                in_=planes.rearrange("p t (c i) -> p c t i", i=RUN),
+            )
+            return woven
+
+        def quantize(name, woven):
+            codes = sbuf(name + "_codes", [P, P], U32)
+            scales = sbuf(name + "_scales", [P, P], U8)
+            nc.vector.quantize_mx(out=codes[:].bitcast(FP8X4), scales=scales[:], in_=woven[:].rearrange("p c t -> p (c t)"))
+            return codes, scales
+
+        def product(result, stationary, moving, moving_dtype):
+            nc.tensor.matmul_mx(
+                out=result,
+                lhsT=stationary[0][:].bitcast(FP8X4),
+                lhsT_scale=stationary[1][:],
+                rhs=moving[0][:].bitcast(moving_dtype),
+                rhs_scale=moving[1][:],
+                start=True,
+                stop=True,
+            )
+
+        def turn_planes(name, planes):
+            turned = psum.tile([P, PACK, P], F32, name=name, tag="turned")
+            for t in range(PACK):
+                nc.tensor.transpose(turned[:, t, :], planes[:, t, :], identity[:])
+            return turned
+
+        warm_in = sbuf("warm_in", [P, 1], F32)
+        nc.gpsimd.memset(warm_in[:], 0.0)
+        warm = sbuf("warm", [P, 1], F32)
+        nc.scalar.activation(out=warm[:], in_=warm_in[:], func=ACT.Exp)
+
+        offsets = keep.tile([P, SLOTS // 16], U16, name="offsets")
+        nc.sync.dma_start(offsets[:], offs)
+        tab_window = sbuf("tab_window", [P, POOL], U16)
+        nc.sync.dma_start(out=tab_window[:].bitcast(I32), in_=tab_words[0].bitcast(I32))
+        tab_scale_window = sbuf("tab_scale_window", [P, POOL], U8)
+        load_scale_rows(tab_scale_window, tab_scales)
+
+        def load_w1(half):
+            raw = sbuf("w1_raw%d" % half, [P, PACK, HIDDEN // 2], F32)
+            nc.sync.dma_start(out=raw[:], in_=w1[:, 256 * half : 256 * (half + 1)].rearrange("(p t) r -> p t r", t=PACK))
+            return raw
+
+        w1_raw = [load_w1(0)]
+        keys_window = sbuf("keys_window", [P, POOL], U16)
+        nc.sync.dma_start(out=keys_window[:].bitcast(I32), in_=keys_words[0].bitcast(I32))
+        keys_scale_window = sbuf("keys_scale_window", [P, POOL], U8)
+        load_scale_rows(keys_scale_window, keys_scales)
+        query_raw = sbuf("query_raw", [P, PACK, P], F32)
+        nc.sync.dma_start(out=query_raw[:], in_=query.rearrange("(p t) q -> p t q", t=PACK))
+        w1_raw.append(load_w1(1))
+
+        temper_sb = sbuf("temper_sb", [P, TILES], F32)
+        with nc.allow_non_contiguous_dma(reason="one temper a partition"):
+            nc.gpsimd.dma_start(out=temper_sb[:], in_=temper.rearrange("(j p) o -> p (j o)", p=P))
+        vs_sb = sbuf("vs_sb", [P, PACK], F32)
+        nc.gpsimd.dma_start(out=vs_sb[:], in_=slot_scale.rearrange("o (p t) -> (o p) t", t=PACK))
+        os_sb = sbuf("os_sb", [P, PACK], F32)
+        nc.gpsimd.dma_start(out=os_sb[:], in_=slot_factor.rearrange("o (p t) -> (o p) t", t=PACK))
+        identity = sbuf("identity", [P, P], F32)
+        make_identity(nc, identity[:])
+
+
+        tab_listed = gather("tab_listed", tab_window, U16)
+        tab_pair = (tab_listed, gather("tab_scales_listed", tab_scale_window, U8))
+
+        exps = []
+
+        def layer(j):
+            raw = w1_raw[j // 2][:, :, P * (j % 2) : P * (j % 2 + 1)]
+            weights = quantize("w1_%d" % j, round_and_weave("w1_woven%d" % j, raw))
+            zh = psum.tile([P, SLOTS], F32, name="zh%d" % j, tag="zh")
+            product(zh[:], weights, tab_pair, FP4X4)
+            ht = sbuf("ht%d" % j, [P, PACK, P], F32)
+            nc.scalar.activation(out=ht[:], in_=zh[:].rearrange("r (s t) -> r t s", t=PACK), func=ACT.Exp, scale=temper_sb[:, j : j + 1])
+            exps.append(ht)
+
+        layer(0)
+        layer(1)
+        keys_listed = gather("keys_listed", keys_window, U16)
+        keys_pair = (keys_listed, gather("keys_scales_listed", keys_scale_window, U8))
+        queries = quantize("query", round_and_weave("query_woven", query_raw[:]))
+        scores = psum.tile([P, SLOTS], F32, name="scores", tag="sums")
+        product(scores[:], queries, keys_pair, FP4X4)
+        layer(2)
+        layer(3)
+
+        neg_max = sbuf("neg_max", [P, 1], F32)
+        nc.vector.tensor_reduce(out=neg_max[:], in_=scores[:], axis=AXIS.X, op=ALU.max, negate=True)
+        probs = sbuf("probs", [P, PACK, P], F32)
+        row_sum = sbuf("row_sum", [P, 1], F32)
+        nc.scalar.activation(
+            out=probs[:], in_=scores[:].rearrange("q (s t) -> q t s", t=PACK), func=ACT.Exp, bias=neg_max[:], accum_out=row_sum[:]
+        )
+
+        def group_sums(j):
+            sums = sbuf("sums%d" % j, [P, GROUPS], F32)
+            nc.vector.tensor_reduce(out=sums[:], in_=exps[j][:].rearrange("r t (g e) -> r g t e", e=2), axis=AXIS.XY, op=ALU.add)
+            return sums
+
+        def scaled_planes(j):
+            turned = turn_planes("ht_turned%d" % j, exps[j])
+            scaled = sbuf("scaled%d" % j, [P, PACK, P], F32)
+            for t in range(PACK):
+                nc.scalar.activation(out=scaled[:, t, :], in_=turned[:, t, :], func=ACT.Copy, scale=vs_sb[:, t : t + 1])
+            return scaled
+
+        def inverse_turned(j, sums):
+            inverse = sbuf("inverse%d" % j, [P, GROUPS], F32)
+            nc.vector.reciprocal(inverse[:], sums[:])
+            doubled = sbuf("doubled%d" % j, [P, GROUPS, 2], F32)
+            nc.scalar.activation(out=doubled[:], in_=inverse[:].unsqueeze(2).to_broadcast([P, GROUPS, 2]), func=ACT.Copy, scale=4.0)
+            turned = psum.tile([P, P], F32, name="inverse_turned%d" % j, tag="inverse")
+            nc.tensor.transpose(turned[:], doubled[:].rearrange("r g e -> r (g e)"), identity[:])
+            return turned
+
+        def values_woven(j, scaled, inverse):
+            woven = sbuf("values_woven%d" % j, [P, P, PACK], BF16)
+            nc.vector.tensor_tensor(
+                out=woven[:].rearrange("p (c i) t -> p c t i", i=RUN),
+                in0=scaled[:].rearrange("p t (c i) -> p c t i", i=RUN),
+                in1=inverse[:].rearrange("p (c i) -> p c i", i=RUN).unsqueeze(2).to_broadcast([P, P // RUN, PACK, RUN]),
+                op=ALU.mult,
+            )
+            return woven
+
+        def read_out(j, woven):
+            values = quantize("values%d" % j, woven)
+            sums = psum.tile([P, P], F32, name="result%d" % j, tag="sums")
+            product(sums[:], weights_mx, values, FP8X4)
+            result = sbuf("result_sb%d" % j, [P, P], F32)
+            nc.scalar.copy(out=result[:], in_=sums[:])
+            nc.sync.dma_start(out=out[:, P * j : P * (j + 1)], in_=result[:])
+
+        sums0 = group_sums(0)
+        scaled0 = scaled_planes(0)
+        inverse0 = inverse_turned(0, sums0)
+        row_inverse = sbuf("row_inverse", [P, 1], F32)
+        nc.vector.reciprocal(row_inverse[:], row_sum[:])
+        normed = sbuf("normed", [P, PACK, P], F32)
+        nc.gpsimd.tensor_scalar(out=normed[:], in0=probs[:], scalar1=row_inverse[:], scalar2=0.0, op0=ALU.mult, op1=ALU.add)
+        sums1 = group_sums(1)
+        scaled1 = scaled_planes(1)
+        inverse1 = inverse_turned(1, sums1)
+        woven0 = values_woven(0, scaled0, inverse0)
+        sums2 = group_sums(2)
+        normed_turned = turn_planes("normed_turned", normed)
+        weights_woven = sbuf("weights_woven", [P, P, PACK], BF16)
+        nc.vector.tensor_tensor(
+            out=weights_woven[:],
+            in0=normed_turned[:].rearrange("p t q -> p q t"),
+            in1=os_sb[:].unsqueeze(1).to_broadcast([P, P, PACK]),
+            op=ALU.mult,
+        )
+        scaled2 = scaled_planes(2)
+        inverse2 = inverse_turned(2, sums2)
+        woven1 = values_woven(1, scaled1, inverse1)
+        weights_mx = quantize("weights", weights_woven)
+        sums3 = group_sums(3)
+        scaled3 = scaled_planes(3)
+        read_out(0, woven0)
+        inverse3 = inverse_turned(3, sums3)
+        read_out(1, woven1)
+        woven2 = values_woven(2, scaled2, inverse2)
+        woven3 = values_woven(3, scaled3, inverse3)
+        read_out(2, woven2)
+        read_out(3, woven3)

@@ -23,6 +23,8 @@ HIDDEN = 512
 TILES = HIDDEN // P
 GROUPS = SLOTS // 8
 RUN = 4
+VECTOR_TILES = 29
+SCALAR_TILES = 22
 
 FLOPS = 2 * 128 * 512 * 512 + 2 * 512 * 512 * 512 + 2 * 128 * 512 * 512
 
@@ -31,26 +33,35 @@ def tile_attend_lrshared_soft_kernel(tc, query, keys_words, keys_scales, tab_wor
     nc = tc.nc
     with ExitStack() as ctx:
         keep = ctx.enter_context(tc.tile_pool(name="keep", bufs=1))
-        psum = ctx.enter_context(tc.psum_pool(name="psum", bufs=2))
+        psum = ctx.enter_context(tc.psum_pool(name="psum", bufs=8))
 
-        def sbuf(name, shape, dtype):
-            return keep.tile(shape, dtype, name=name, align_bytes=64)
+        def sbuf(name, shape, dtype, tag=None):
+            return keep.tile(shape, dtype, name=name, tag=tag or name, align_bytes=64)
 
-        def load_scale_rows(window, scales):
+        def vector_tile(name, shape, dtype):
+            return keep.tile(shape, dtype, name=name, tag="vector_out", bufs=VECTOR_TILES, align_bytes=64)
+
+        def scalar_tile(name, shape, dtype):
+            return keep.tile(shape, dtype, name=name, tag="scalar_out", bufs=SCALAR_TILES, align_bytes=64)
+
+        def bank(name, shape):
+            return psum.tile(shape, F32, name=name, tag="bank")
+
+        def load_scale_rows(window, scales, queue):
             nc.vector.memset(window[:].bitcast(I32), 0)
             for quadrant in range(4):
-                nc.sync.dma_start(
+                queue.dma_start(
                     out=window[32 * quadrant : 32 * quadrant + 4, :].bitcast(I32),
                     in_=scales[0, 4 * quadrant : 4 * quadrant + 4, :].bitcast(I32),
                 )
 
         def gather(name, window, dtype):
-            listed = sbuf(name, [P, SLOTS], dtype)
+            listed = vector_tile(name, [P, SLOTS], dtype)
             nc.vector.tensor_copy(listed[:], window[:].indirect(offsets[:]))
             return listed
 
         def round_and_weave(name, planes):
-            woven = sbuf(name, [P, P, PACK], BF16)
+            woven = scalar_tile(name, [P, P, PACK], BF16)
             nc.scalar.copy(
                 out=woven[:].rearrange("p (c i) t -> p c t i", i=RUN),
                 in_=planes.rearrange("p t (c i) -> p c t i", i=RUN),
@@ -58,7 +69,7 @@ def tile_attend_lrshared_soft_kernel(tc, query, keys_words, keys_scales, tab_wor
             return woven
 
         def quantize(name, woven):
-            codes = sbuf(name + "_codes", [P, P], U32)
+            codes = vector_tile(name + "_codes", [P, P], U32)
             scales = sbuf(name + "_scales", [P, P], U8)
             nc.vector.quantize_mx(out=codes[:].bitcast(FP8X4), scales=scales[:], in_=woven[:].rearrange("p c t -> p (c t)"))
             return codes, scales
@@ -75,22 +86,21 @@ def tile_attend_lrshared_soft_kernel(tc, query, keys_words, keys_scales, tab_wor
             )
 
         def turn_planes(name, planes):
-            turned = psum.tile([P, PACK, P], F32, name=name, tag="turned")
+            turned = bank(name, [P, PACK, P])
             for t in range(PACK):
                 nc.tensor.transpose(turned[:, t, :], planes[:, t, :], identity[:])
             return turned
-
-        warm_in = sbuf("warm_in", [P, 1], F32)
-        nc.gpsimd.memset(warm_in[:], 0.0)
-        warm = sbuf("warm", [P, 1], F32)
-        nc.scalar.activation(out=warm[:], in_=warm_in[:], func=ACT.Exp)
 
         offsets = keep.tile([P, SLOTS // 16], U16, name="offsets")
         nc.sync.dma_start(offsets[:], offs)
         tab_window = sbuf("tab_window", [P, POOL], U16)
         nc.sync.dma_start(out=tab_window[:].bitcast(I32), in_=tab_words[0].bitcast(I32))
         tab_scale_window = sbuf("tab_scale_window", [P, POOL], U8)
-        load_scale_rows(tab_scale_window, tab_scales)
+        load_scale_rows(tab_scale_window, tab_scales, nc.sync)
+        warm_in = sbuf("warm_in", [P, 1], F32)
+        nc.gpsimd.memset(warm_in[:], 0.0)
+        warm = sbuf("warm", [P, 1], F32)
+        nc.scalar.activation(out=warm[:], in_=warm_in[:], func=ACT.Exp)
 
         def load_w1(half):
             raw = sbuf("w1_raw%d" % half, [P, PACK, HIDDEN // 2], F32)
@@ -101,10 +111,10 @@ def tile_attend_lrshared_soft_kernel(tc, query, keys_words, keys_scales, tab_wor
         keys_window = sbuf("keys_window", [P, POOL], U16)
         nc.sync.dma_start(out=keys_window[:].bitcast(I32), in_=keys_words[0].bitcast(I32))
         keys_scale_window = sbuf("keys_scale_window", [P, POOL], U8)
-        load_scale_rows(keys_scale_window, keys_scales)
+        load_scale_rows(keys_scale_window, keys_scales, nc.sync)
+        w1_raw.append(load_w1(1))
         query_raw = sbuf("query_raw", [P, PACK, P], F32)
         nc.sync.dma_start(out=query_raw[:], in_=query.rearrange("(p t) q -> p t q", t=PACK))
-        w1_raw.append(load_w1(1))
 
         temper_sb = sbuf("temper_sb", [P, TILES], F32)
         with nc.allow_non_contiguous_dma(reason="one temper a partition"):
@@ -117,61 +127,47 @@ def tile_attend_lrshared_soft_kernel(tc, query, keys_words, keys_scales, tab_wor
         make_identity(nc, identity[:])
 
 
-        tab_listed = gather("tab_listed", tab_window, U16)
-        tab_pair = (tab_listed, gather("tab_scales_listed", tab_scale_window, U8))
+        def w1_woven(j):
+            return round_and_weave("w1_woven%d" % j, w1_raw[j // 2][:, :, P * (j % 2) : P * (j % 2 + 1)])
 
-        exps = []
-
-        def layer(j):
-            raw = w1_raw[j // 2][:, :, P * (j % 2) : P * (j % 2 + 1)]
-            weights = quantize("w1_%d" % j, round_and_weave("w1_woven%d" % j, raw))
-            zh = psum.tile([P, SLOTS], F32, name="zh%d" % j, tag="zh")
-            product(zh[:], weights, tab_pair, FP4X4)
-            ht = sbuf("ht%d" % j, [P, PACK, P], F32)
-            nc.scalar.activation(out=ht[:], in_=zh[:].rearrange("r (s t) -> r t s", t=PACK), func=ACT.Exp, scale=temper_sb[:, j : j + 1])
-            exps.append(ht)
-
-        layer(0)
-        layer(1)
-        keys_listed = gather("keys_listed", keys_window, U16)
-        keys_pair = (keys_listed, gather("keys_scales_listed", keys_scale_window, U8))
-        queries = quantize("query", round_and_weave("query_woven", query_raw[:]))
-        scores = psum.tile([P, SLOTS], F32, name="scores", tag="sums")
-        product(scores[:], queries, keys_pair, FP4X4)
-        layer(2)
-        layer(3)
-
-        neg_max = sbuf("neg_max", [P, 1], F32)
-        nc.vector.tensor_reduce(out=neg_max[:], in_=scores[:], axis=AXIS.X, op=ALU.max, negate=True)
-        probs = sbuf("probs", [P, PACK, P], F32)
-        row_sum = sbuf("row_sum", [P, 1], F32)
-        nc.scalar.activation(
-            out=probs[:], in_=scores[:].rearrange("q (s t) -> q t s", t=PACK), func=ACT.Exp, bias=neg_max[:], accum_out=row_sum[:]
-        )
-
-        def group_sums(j):
-            sums = sbuf("sums%d" % j, [P, GROUPS], F32)
-            nc.vector.tensor_reduce(out=sums[:], in_=exps[j][:].rearrange("r t (g e) -> r g t e", e=2), axis=AXIS.XY, op=ALU.add)
+        def listed_product(name, stationary, listed):
+            sums = bank(name, [P, SLOTS])
+            product(sums[:], stationary, listed, FP4X4)
             return sums
 
-        def scaled_planes(j):
-            turned = turn_planes("ht_turned%d" % j, exps[j])
-            scaled = sbuf("scaled%d" % j, [P, PACK, P], F32)
+        def exponentials(j, zh):
+            ht = scalar_tile("ht%d" % j, [P, PACK, P], F32)
+            nc.scalar.activation(out=ht[:], in_=zh[:].rearrange("r (s t) -> r t s", t=PACK), func=ACT.Exp, scale=temper_sb[:, j : j + 1])
+            return ht
+
+        def group_sums(j, ht):
+            sums = vector_tile("sums%d" % j, [P, GROUPS], F32)
+            nc.vector.tensor_reduce(out=sums[:], in_=ht[:].rearrange("r t (g e) -> r g t e", e=2), axis=AXIS.XY, op=ALU.add)
+            return sums
+
+        def scaled_planes(j, turned):
+            scaled = scalar_tile("scaled%d" % j, [P, PACK, P], F32)
             for t in range(PACK):
                 nc.scalar.activation(out=scaled[:, t, :], in_=turned[:, t, :], func=ACT.Copy, scale=vs_sb[:, t : t + 1])
             return scaled
 
-        def inverse_turned(j, sums):
-            inverse = sbuf("inverse%d" % j, [P, GROUPS], F32)
+        def inverse_of(name, sums, width):
+            inverse = vector_tile(name, [P, width], F32)
             nc.vector.reciprocal(inverse[:], sums[:])
-            doubled = sbuf("doubled%d" % j, [P, GROUPS, 2], F32)
-            nc.scalar.activation(out=doubled[:], in_=inverse[:].unsqueeze(2).to_broadcast([P, GROUPS, 2]), func=ACT.Copy, scale=4.0)
-            turned = psum.tile([P, P], F32, name="inverse_turned%d" % j, tag="inverse")
-            nc.tensor.transpose(turned[:], doubled[:].rearrange("r g e -> r (g e)"), identity[:])
+            return inverse
+
+        def doubled(j, inverse):
+            twice = scalar_tile("doubled%d" % j, [P, GROUPS, 2], F32)
+            nc.scalar.activation(out=twice[:], in_=inverse[:].unsqueeze(2).to_broadcast([P, GROUPS, 2]), func=ACT.Copy, scale=4.0)
+            return twice
+
+        def turn_inverse(j, twice):
+            turned = bank("inverse_turned%d" % j, [P, P])
+            nc.tensor.transpose(turned[:], twice[:].rearrange("r g e -> r (g e)"), identity[:])
             return turned
 
         def values_woven(j, scaled, inverse):
-            woven = sbuf("values_woven%d" % j, [P, P, PACK], BF16)
+            woven = vector_tile("values_woven%d" % j, [P, P, PACK], BF16)
             nc.vector.tensor_tensor(
                 out=woven[:].rearrange("p (c i) t -> p c t i", i=RUN),
                 in0=scaled[:].rearrange("p t (c i) -> p c t i", i=RUN),
@@ -180,44 +176,104 @@ def tile_attend_lrshared_soft_kernel(tc, query, keys_words, keys_scales, tab_wor
             )
             return woven
 
-        def read_out(j, woven):
-            values = quantize("values%d" % j, woven)
-            sums = psum.tile([P, P], F32, name="result%d" % j, tag="sums")
+        def read_out(j, values, weights_mx):
+            sums = bank("result%d" % j, [P, P])
             product(sums[:], weights_mx, values, FP8X4)
-            result = sbuf("result_sb%d" % j, [P, P], F32)
+            result = scalar_tile("result_sb%d" % j, [P, P], F32)
             nc.scalar.copy(out=result[:], in_=sums[:])
             nc.sync.dma_start(out=out[:, P * j : P * (j + 1)], in_=result[:])
 
-        sums0 = group_sums(0)
-        scaled0 = scaled_planes(0)
-        inverse0 = inverse_turned(0, sums0)
-        row_inverse = sbuf("row_inverse", [P, 1], F32)
-        nc.vector.reciprocal(row_inverse[:], row_sum[:])
-        normed = sbuf("normed", [P, PACK, P], F32)
-        nc.gpsimd.tensor_scalar(out=normed[:], in0=probs[:], scalar1=row_inverse[:], scalar2=0.0, op0=ALU.mult, op1=ALU.add)
-        sums1 = group_sums(1)
-        scaled1 = scaled_planes(1)
-        inverse1 = inverse_turned(1, sums1)
-        woven0 = values_woven(0, scaled0, inverse0)
-        sums2 = group_sums(2)
+        def negated_max(scores):
+            neg_max = vector_tile("neg_max", [P, 1], F32)
+            nc.vector.tensor_reduce(out=neg_max[:], in_=scores[:], axis=AXIS.X, op=ALU.max, negate=True)
+            return neg_max
+
+        def softmax_terms(scores, neg_max):
+            probs = scalar_tile("probs", [P, PACK, P], F32)
+            row_sum = sbuf("row_sum", [P, 1], F32)
+            nc.scalar.activation(
+                out=probs[:], in_=scores[:].rearrange("q (s t) -> q t s", t=PACK), func=ACT.Exp, bias=neg_max[:], accum_out=row_sum[:]
+            )
+            return probs, row_sum
+
+        def normalise(probs, row_inverse):
+            normed = sbuf("normed", [P, PACK, P], F32)
+            nc.gpsimd.tensor_scalar(out=normed[:], in0=probs[:], scalar1=row_inverse[:], scalar2=0.0, op0=ALU.mult, op1=ALU.add)
+            return normed
+
+        def weights_woven(turned):
+            woven = vector_tile("weights_woven", [P, P, PACK], BF16)
+            nc.vector.tensor_tensor(
+                out=woven[:],
+                in0=turned[:].rearrange("p t q -> p q t"),
+                in1=os_sb[:].unsqueeze(1).to_broadcast([P, P, PACK]),
+                op=ALU.mult,
+            )
+            return woven
+
+        tab_listed = gather("tab_listed", tab_window, U16)
+        tab_pair = (tab_listed, gather("tab_scales_listed", tab_scale_window, U8))
+        w1_bf0 = w1_woven(0)
+        w1_bf1 = w1_woven(1)
+        w1_mx0 = quantize("w1_0", w1_bf0)
+        zh0 = listed_product("zh0", w1_mx0, tab_pair)
+        w1_mx1 = quantize("w1_1", w1_bf1)
+        zh1 = listed_product("zh1", w1_mx1, tab_pair)
+        keys_listed = gather("keys_listed", keys_window, U16)
+        w1_bf2 = w1_woven(2)
+        ht0 = exponentials(0, zh0)
+        keys_pair = (keys_listed, gather("keys_scales_listed", keys_scale_window, U8))
+        query_bf = round_and_weave("query_woven", query_raw[:])
+        turned0 = turn_planes("ht_turned0", ht0)
+        w1_mx2 = quantize("w1_2", w1_bf2)
+        zh2 = listed_product("zh2", w1_mx2, tab_pair)
+        w1_bf3 = w1_woven(3)
+        sums0 = group_sums(0, ht0)
+        queries = quantize("query", query_bf)
+        scores = listed_product("scores", queries, keys_pair)
+        ht1 = exponentials(1, zh1)
+        w1_mx3 = quantize("w1_3", w1_bf3)
+        zh3 = listed_product("zh3", w1_mx3, tab_pair)
+        inverse0 = inverse_of("inverse0", sums0, GROUPS)
+        turned1 = turn_planes("ht_turned1", ht1)
+        ht2 = exponentials(2, zh2)
+        sums1 = group_sums(1, ht1)
+        scaled0 = scaled_planes(0, turned0)
+        twice0 = doubled(0, inverse0)
+        neg_max = negated_max(scores)
+        inverse_turned0 = turn_inverse(0, twice0)
+        probs, row_sum = softmax_terms(scores, neg_max)
+        ht3 = exponentials(3, zh3)
+        inverse1 = inverse_of("inverse1", sums1, GROUPS)
+        turned2 = turn_planes("ht_turned2", ht2)
+        sums2 = group_sums(2, ht2)
+        twice1 = doubled(1, inverse1)
+        inverse_turned1 = turn_inverse(1, twice1)
+        woven0 = values_woven(0, scaled0, inverse_turned0)
+        row_inverse = inverse_of("row_inverse", row_sum, 1)
+        normed = normalise(probs, row_inverse)
+        scaled1 = scaled_planes(1, turned1)
+        inverse2 = inverse_of("inverse2", sums2, GROUPS)
+        turned3 = turn_planes("ht_turned3", ht3)
+        sums3 = group_sums(3, ht3)
+        scaled2 = scaled_planes(2, turned2)
+        twice2 = doubled(2, inverse2)
         normed_turned = turn_planes("normed_turned", normed)
-        weights_woven = sbuf("weights_woven", [P, P, PACK], BF16)
-        nc.vector.tensor_tensor(
-            out=weights_woven[:],
-            in0=normed_turned[:].rearrange("p t q -> p q t"),
-            in1=os_sb[:].unsqueeze(1).to_broadcast([P, P, PACK]),
-            op=ALU.mult,
-        )
-        scaled2 = scaled_planes(2)
-        inverse2 = inverse_turned(2, sums2)
-        woven1 = values_woven(1, scaled1, inverse1)
-        weights_mx = quantize("weights", weights_woven)
-        sums3 = group_sums(3)
-        scaled3 = scaled_planes(3)
-        read_out(0, woven0)
-        inverse3 = inverse_turned(3, sums3)
-        read_out(1, woven1)
-        woven2 = values_woven(2, scaled2, inverse2)
-        woven3 = values_woven(3, scaled3, inverse3)
-        read_out(2, woven2)
-        read_out(3, woven3)
+        inverse_turned2 = turn_inverse(2, twice2)
+        woven1 = values_woven(1, scaled1, inverse_turned1)
+        inverse3 = inverse_of("inverse3", sums3, GROUPS)
+        scaled3 = scaled_planes(3, turned3)
+        twice3 = doubled(3, inverse3)
+        weights_bf = weights_woven(normed_turned)
+        inverse_turned3 = turn_inverse(3, twice3)
+        values0 = quantize("values0", woven0)
+        woven2 = values_woven(2, scaled2, inverse_turned2)
+        weights_mx = quantize("weights", weights_bf)
+        read_out(0, values0, weights_mx)
+        values1 = quantize("values1", woven1)
+        read_out(1, values1, weights_mx)
+        woven3 = values_woven(3, scaled3, inverse_turned3)
+        values2 = quantize("values2", woven2)
+        read_out(2, values2, weights_mx)
+        values3 = quantize("values3", woven3)
+        read_out(3, values3, weights_mx)

@@ -24,7 +24,7 @@ TILES = HIDDEN // P
 GROUPS = SLOTS // 8
 RUN = 4
 VECTOR_TILES = 29
-SCALAR_TILES = 22
+SCALAR_TILES = 23
 
 FLOPS = 2 * 128 * 512 * 512 + 2 * 512 * 512 * 512 + 2 * 128 * 512 * 512
 
@@ -91,44 +91,44 @@ def tile_attend_lrshared_soft_kernel(tc, query, keys_words, keys_scales, tab_wor
                 nc.tensor.transpose(turned[:, t, :], planes[:, t, :], identity[:])
             return turned
 
-        offsets = keep.tile([P, SLOTS // 16], U16, name="offsets")
-        nc.sync.dma_start(offsets[:], offs)
         tab_window = sbuf("tab_window", [P, POOL], U16)
         nc.sync.dma_start(out=tab_window[:].bitcast(I32), in_=tab_words[0].bitcast(I32))
+        offsets = keep.tile([P, SLOTS // 16], U16, name="offsets")
+        nc.sync.dma_start(offsets[:], offs)
         tab_scale_window = sbuf("tab_scale_window", [P, POOL], U8)
         load_scale_rows(tab_scale_window, tab_scales, nc.sync)
+
+        def load_w1(first, count):
+            raw = sbuf("w1_raw%d" % first, [P, PACK, P * count], F32)
+            nc.sync.dma_start(out=raw[:], in_=w1[:, P * first : P * (first + count)].rearrange("(p t) r -> p t r", t=PACK))
+            return [raw[:, :, P * j : P * (j + 1)] for j in range(count)]
+
+        w1_raw = load_w1(0, 2)
+        keys_window = sbuf("keys_window", [P, POOL], U16)
+        nc.sync.dma_start(out=keys_window[:].bitcast(I32), in_=keys_words[0].bitcast(I32))
+        keys_scale_window = sbuf("keys_scale_window", [P, POOL], U8)
+        load_scale_rows(keys_scale_window, keys_scales, nc.sync)
+        w1_raw.extend(load_w1(2, 2))
+        query_raw = sbuf("query_raw", [P, PACK, P], F32)
+        nc.sync.dma_start(out=query_raw[:], in_=query.rearrange("(p t) q -> p t q", t=PACK))
+
         warm_in = sbuf("warm_in", [P, 1], F32)
         nc.gpsimd.memset(warm_in[:], 0.0)
         warm = sbuf("warm", [P, 1], F32)
         nc.scalar.activation(out=warm[:], in_=warm_in[:], func=ACT.Exp)
 
-        def load_w1(half):
-            raw = sbuf("w1_raw%d" % half, [P, PACK, HIDDEN // 2], F32)
-            nc.sync.dma_start(out=raw[:], in_=w1[:, 256 * half : 256 * (half + 1)].rearrange("(p t) r -> p t r", t=PACK))
-            return raw
-
-        w1_raw = [load_w1(0)]
-        keys_window = sbuf("keys_window", [P, POOL], U16)
-        nc.sync.dma_start(out=keys_window[:].bitcast(I32), in_=keys_words[0].bitcast(I32))
-        keys_scale_window = sbuf("keys_scale_window", [P, POOL], U8)
-        load_scale_rows(keys_scale_window, keys_scales, nc.sync)
-        w1_raw.append(load_w1(1))
-        query_raw = sbuf("query_raw", [P, PACK, P], F32)
-        nc.sync.dma_start(out=query_raw[:], in_=query.rearrange("(p t) q -> p t q", t=PACK))
-
-        temper_sb = sbuf("temper_sb", [P, TILES], F32)
-        with nc.allow_non_contiguous_dma(reason="one temper a partition"):
-            nc.gpsimd.dma_start(out=temper_sb[:], in_=temper.rearrange("(j p) o -> p (j o)", p=P))
+        temper_rows = sbuf("temper_rows", [P, P], F32)
+        nc.gpsimd.memset(temper_rows[:], 0.0)
+        nc.gpsimd.dma_start(out=temper_rows[0:TILES, :], in_=temper.rearrange("(j m) o -> j (m o)", m=P))
+        identity = sbuf("identity", [P, P], F32)
+        make_identity(nc, identity[:])
         vs_sb = sbuf("vs_sb", [P, PACK], F32)
         nc.gpsimd.dma_start(out=vs_sb[:], in_=slot_scale.rearrange("o (p t) -> (o p) t", t=PACK))
         os_sb = sbuf("os_sb", [P, PACK], F32)
         nc.gpsimd.dma_start(out=os_sb[:], in_=slot_factor.rearrange("o (p t) -> (o p) t", t=PACK))
-        identity = sbuf("identity", [P, P], F32)
-        make_identity(nc, identity[:])
-
 
         def w1_woven(j):
-            return round_and_weave("w1_woven%d" % j, w1_raw[j // 2][:, :, P * (j % 2) : P * (j % 2 + 1)])
+            return round_and_weave("w1_woven%d" % j, w1_raw[j])
 
         def listed_product(name, stationary, listed):
             sums = bank(name, [P, SLOTS])
@@ -211,29 +211,47 @@ def tile_attend_lrshared_soft_kernel(tc, query, keys_words, keys_scales, tab_wor
             )
             return woven
 
+        def factored_planes(turned):
+            planes = scalar_tile("weights_planes", [P, PACK, P], BF16)
+            for t in range(PACK):
+                nc.scalar.activation(out=planes[:, t, :], in_=turned[:, t, :], func=ACT.Copy, scale=os_sb[:, t : t + 1])
+            return planes
+
+        def turn_temper():
+            turned = bank("temper_turned", [P, P])
+            nc.tensor.transpose(turned[:], temper_rows[:], identity[:])
+            return turned
+
+        def temper_columns(turned):
+            columns = scalar_tile("temper_sb", [P, TILES], F32)
+            nc.scalar.copy(out=columns[:], in_=turned[:, 0:TILES])
+            return columns
+
         tab_listed = gather("tab_listed", tab_window, U16)
-        tab_pair = (tab_listed, gather("tab_scales_listed", tab_scale_window, U8))
+        tab_bytes = gather("tab_scales_listed", tab_scale_window, U8)
         w1_bf0 = w1_woven(0)
         w1_bf1 = w1_woven(1)
+        temper_turned = turn_temper()
+        temper_sb = temper_columns(temper_turned)
         w1_mx0 = quantize("w1_0", w1_bf0)
-        zh0 = listed_product("zh0", w1_mx0, tab_pair)
-        w1_mx1 = quantize("w1_1", w1_bf1)
-        zh1 = listed_product("zh1", w1_mx1, tab_pair)
+        zh0 = listed_product("zh0", w1_mx0, (tab_listed, tab_bytes))
         keys_listed = gather("keys_listed", keys_window, U16)
-        w1_bf2 = w1_woven(2)
+        w1_mx1 = quantize("w1_1", w1_bf1)
+        zh1 = listed_product("zh1", w1_mx1, (tab_listed, tab_bytes))
         ht0 = exponentials(0, zh0)
-        keys_pair = (keys_listed, gather("keys_scales_listed", keys_scale_window, U8))
+        w1_bf2 = w1_woven(2)
+        keys_bytes = gather("keys_scales_listed", keys_scale_window, U8)
         query_bf = round_and_weave("query_woven", query_raw[:])
         turned0 = turn_planes("ht_turned0", ht0)
-        w1_mx2 = quantize("w1_2", w1_bf2)
-        zh2 = listed_product("zh2", w1_mx2, tab_pair)
-        w1_bf3 = w1_woven(3)
         sums0 = group_sums(0, ht0)
+        w1_mx2 = quantize("w1_2", w1_bf2)
+        zh2 = listed_product("zh2", w1_mx2, (tab_listed, tab_bytes))
+        w1_bf3 = w1_woven(3)
         queries = quantize("query", query_bf)
-        scores = listed_product("scores", queries, keys_pair)
+        scores = listed_product("scores", queries, (keys_listed, keys_bytes))
         ht1 = exponentials(1, zh1)
         w1_mx3 = quantize("w1_3", w1_bf3)
-        zh3 = listed_product("zh3", w1_mx3, tab_pair)
+        zh3 = listed_product("zh3", w1_mx3, (tab_listed, tab_bytes))
         inverse0 = inverse_of("inverse0", sums0, GROUPS)
         turned1 = turn_planes("ht_turned1", ht1)
         ht2 = exponentials(2, zh2)

@@ -23,8 +23,8 @@ HIDDEN = 512
 TILES = HIDDEN // P
 GROUPS = SLOTS // 8
 RUN = 4
-VECTOR_TILES = 29
-SCALAR_TILES = 23
+VECTOR_TILES = 28
+SCALAR_TILES = 21
 
 FLOPS = 2 * 128 * 512 * 512 + 2 * 512 * 512 * 512 + 2 * 128 * 512 * 512
 
@@ -104,18 +104,13 @@ def tile_attend_lrshared_soft_kernel(tc, query, keys_words, keys_scales, tab_wor
             return [raw[:, :, P * j : P * (j + 1)] for j in range(count)]
 
         w1_raw = load_w1(0, 2)
+        query_raw = sbuf("query_raw", [P, PACK, P], F32)
+        nc.sync.dma_start(out=query_raw[:], in_=query.rearrange("(p t) q -> p t q", t=PACK))
         keys_window = sbuf("keys_window", [P, POOL], U16)
         nc.sync.dma_start(out=keys_window[:].bitcast(I32), in_=keys_words[0].bitcast(I32))
         keys_scale_window = sbuf("keys_scale_window", [P, POOL], U8)
         load_scale_rows(keys_scale_window, keys_scales, nc.sync)
         w1_raw.extend(load_w1(2, 2))
-        query_raw = sbuf("query_raw", [P, PACK, P], F32)
-        nc.sync.dma_start(out=query_raw[:], in_=query.rearrange("(p t) q -> p t q", t=PACK))
-
-        warm_in = sbuf("warm_in", [P, 1], F32)
-        nc.gpsimd.memset(warm_in[:], 0.0)
-        warm = sbuf("warm", [P, 1], F32)
-        nc.scalar.activation(out=warm[:], in_=warm_in[:], func=ACT.Exp)
 
         temper_rows = sbuf("temper_rows", [P, P], F32)
         nc.gpsimd.memset(temper_rows[:], 0.0)
@@ -157,8 +152,10 @@ def tile_attend_lrshared_soft_kernel(tc, query, keys_words, keys_scales, tab_wor
             return inverse
 
         def doubled(j, inverse):
-            twice = scalar_tile("doubled%d" % j, [P, GROUPS, 2], F32)
-            nc.scalar.activation(out=twice[:], in_=inverse[:].unsqueeze(2).to_broadcast([P, GROUPS, 2]), func=ACT.Copy, scale=4.0)
+            twice = sbuf("doubled%d" % j, [P, GROUPS, 2], F32)
+            nc.gpsimd.tensor_scalar(
+                out=twice[:], in0=inverse[:].unsqueeze(2).to_broadcast([P, GROUPS, 2]), scalar1=4.0, scalar2=0.0, op0=ALU.mult, op1=ALU.add
+            )
             return twice
 
         def turn_inverse(j, twice):
@@ -231,64 +228,65 @@ def tile_attend_lrshared_soft_kernel(tc, query, keys_words, keys_scales, tab_wor
         tab_bytes = gather("tab_scales_listed", tab_scale_window, U8)
         w1_bf0 = w1_woven(0)
         w1_bf1 = w1_woven(1)
+        query_bf = round_and_weave("query_woven", query_raw[:])
         temper_turned = turn_temper()
         temper_sb = temper_columns(temper_turned)
         w1_mx0 = quantize("w1_0", w1_bf0)
         zh0 = listed_product("zh0", w1_mx0, (tab_listed, tab_bytes))
-        keys_listed = gather("keys_listed", keys_window, U16)
         w1_mx1 = quantize("w1_1", w1_bf1)
         zh1 = listed_product("zh1", w1_mx1, (tab_listed, tab_bytes))
+        keys_listed = gather("keys_listed", keys_window, U16)
         ht0 = exponentials(0, zh0)
+        queries = quantize("query", query_bf)
         w1_bf2 = w1_woven(2)
-        keys_bytes = gather("keys_scales_listed", keys_scale_window, U8)
-        query_bf = round_and_weave("query_woven", query_raw[:])
         turned0 = turn_planes("ht_turned0", ht0)
+        keys_bytes = gather("keys_scales_listed", keys_scale_window, U8)
+        scores = listed_product("scores", queries, (keys_listed, keys_bytes))
+        w1_bf3 = w1_woven(3)
         sums0 = group_sums(0, ht0)
         w1_mx2 = quantize("w1_2", w1_bf2)
         zh2 = listed_product("zh2", w1_mx2, (tab_listed, tab_bytes))
-        w1_bf3 = w1_woven(3)
-        queries = quantize("query", query_bf)
-        scores = listed_product("scores", queries, (keys_listed, keys_bytes))
         ht1 = exponentials(1, zh1)
         w1_mx3 = quantize("w1_3", w1_bf3)
         zh3 = listed_product("zh3", w1_mx3, (tab_listed, tab_bytes))
-        inverse0 = inverse_of("inverse0", sums0, GROUPS)
-        turned1 = turn_planes("ht_turned1", ht1)
-        ht2 = exponentials(2, zh2)
-        sums1 = group_sums(1, ht1)
         scaled0 = scaled_planes(0, turned0)
+        inverse0 = inverse_of("inverse0", sums0, GROUPS)
         twice0 = doubled(0, inverse0)
         neg_max = negated_max(scores)
-        inverse_turned0 = turn_inverse(0, twice0)
+        turned1 = turn_planes("ht_turned1", ht1)
+        ht2 = exponentials(2, zh2)
         probs, row_sum = softmax_terms(scores, neg_max)
-        ht3 = exponentials(3, zh3)
-        inverse1 = inverse_of("inverse1", sums1, GROUPS)
+        sums1 = group_sums(1, ht1)
+        inverse_turned0 = turn_inverse(0, twice0)
         turned2 = turn_planes("ht_turned2", ht2)
+        ht3 = exponentials(3, zh3)
         sums2 = group_sums(2, ht2)
-        twice1 = doubled(1, inverse1)
-        inverse_turned1 = turn_inverse(1, twice1)
-        woven0 = values_woven(0, scaled0, inverse_turned0)
+        scaled1 = scaled_planes(1, turned1)
         row_inverse = inverse_of("row_inverse", row_sum, 1)
         normed = normalise(probs, row_inverse)
-        scaled1 = scaled_planes(1, turned1)
-        inverse2 = inverse_of("inverse2", sums2, GROUPS)
+        inverse1 = inverse_of("inverse1", sums1, GROUPS)
+        twice1 = doubled(1, inverse1)
         turned3 = turn_planes("ht_turned3", ht3)
-        sums3 = group_sums(3, ht3)
+        woven0 = values_woven(0, scaled0, inverse_turned0)
         scaled2 = scaled_planes(2, turned2)
-        twice2 = doubled(2, inverse2)
         normed_turned = turn_planes("normed_turned", normed)
-        inverse_turned2 = turn_inverse(2, twice2)
-        woven1 = values_woven(1, scaled1, inverse_turned1)
-        inverse3 = inverse_of("inverse3", sums3, GROUPS)
+        inverse2 = inverse_of("inverse2", sums2, GROUPS)
+        twice2 = doubled(2, inverse2)
+        inverse_turned1 = turn_inverse(1, twice1)
+        sums3 = group_sums(3, ht3)
         scaled3 = scaled_planes(3, turned3)
-        twice3 = doubled(3, inverse3)
-        weights_bf = weights_woven(normed_turned)
-        inverse_turned3 = turn_inverse(3, twice3)
         values0 = quantize("values0", woven0)
+        inverse_turned2 = turn_inverse(2, twice2)
+        inverse3 = inverse_of("inverse3", sums3, GROUPS)
+        twice3 = doubled(3, inverse3)
+        weights_planes = factored_planes(normed_turned)
+        woven1 = values_woven(1, scaled1, inverse_turned1)
+        weights_bf = round_and_weave("weights_woven", weights_planes[:])
+        inverse_turned3 = turn_inverse(3, twice3)
         woven2 = values_woven(2, scaled2, inverse_turned2)
+        values1 = quantize("values1", woven1)
         weights_mx = quantize("weights", weights_bf)
         read_out(0, values0, weights_mx)
-        values1 = quantize("values1", woven1)
         read_out(1, values1, weights_mx)
         woven3 = values_woven(3, scaled3, inverse_turned3)
         values2 = quantize("values2", woven2)

@@ -23,6 +23,7 @@ HIDDEN = 512
 TILES = HIDDEN // P
 GROUPS = SLOTS // 8
 RUN = 4
+LINE = 2
 VECTOR_TILES = 28
 SCALAR_TILES = 21
 
@@ -104,10 +105,10 @@ def tile_attend_lrshared_soft_kernel(tc, query, keys_words, keys_scales, tab_wor
             return [raw[:, :, P * j : P * (j + 1)] for j in range(count)]
 
         w1_raw = load_w1(0, 2)
-        query_raw = sbuf("query_raw", [P, PACK, P], F32)
-        nc.sync.dma_start(out=query_raw[:], in_=query.rearrange("(p t) q -> p t q", t=PACK))
         keys_window = sbuf("keys_window", [P, POOL], U16)
         nc.sync.dma_start(out=keys_window[:].bitcast(I32), in_=keys_words[0].bitcast(I32))
+        query_raw = sbuf("query_raw", [P, PACK, P], F32)
+        nc.sync.dma_start(out=query_raw[:], in_=query.rearrange("(p t) q -> p t q", t=PACK))
         keys_scale_window = sbuf("keys_scale_window", [P, POOL], U8)
         load_scale_rows(keys_scale_window, keys_scales, nc.sync)
         w1_raw.extend(load_w1(2, 2))
@@ -166,9 +167,9 @@ def tile_attend_lrshared_soft_kernel(tc, query, keys_words, keys_scales, tab_wor
         def values_woven(j, scaled, inverse):
             woven = vector_tile("values_woven%d" % j, [P, P, PACK], BF16)
             nc.vector.tensor_tensor(
-                out=woven[:].rearrange("p (c i) t -> p c t i", i=RUN),
-                in0=scaled[:].rearrange("p t (c i) -> p c t i", i=RUN),
-                in1=inverse[:].rearrange("p (c i) -> p c i", i=RUN).unsqueeze(2).to_broadcast([P, P // RUN, PACK, RUN]),
+                out=woven[:].rearrange("p (c i) t -> p c t i", i=LINE),
+                in0=scaled[:].rearrange("p t (c i) -> p c t i", i=LINE),
+                in1=inverse[:].rearrange("p (c i) -> p c i", i=LINE).unsqueeze(2).to_broadcast([P, P // LINE, PACK, LINE]),
                 op=ALU.mult,
             )
             return woven
@@ -228,14 +229,14 @@ def tile_attend_lrshared_soft_kernel(tc, query, keys_words, keys_scales, tab_wor
         tab_bytes = gather("tab_scales_listed", tab_scale_window, U8)
         w1_bf0 = w1_woven(0)
         w1_bf1 = w1_woven(1)
-        query_bf = round_and_weave("query_woven", query_raw[:])
         temper_turned = turn_temper()
         temper_sb = temper_columns(temper_turned)
         w1_mx0 = quantize("w1_0", w1_bf0)
         zh0 = listed_product("zh0", w1_mx0, (tab_listed, tab_bytes))
+        keys_listed = gather("keys_listed", keys_window, U16)
+        query_bf = round_and_weave("query_woven", query_raw[:])
         w1_mx1 = quantize("w1_1", w1_bf1)
         zh1 = listed_product("zh1", w1_mx1, (tab_listed, tab_bytes))
-        keys_listed = gather("keys_listed", keys_window, U16)
         ht0 = exponentials(0, zh0)
         queries = quantize("query", query_bf)
         w1_bf2 = w1_woven(2)

from contextlib import ExitStack

import concourse.mybir as mybir
from concourse.masks import make_identity

F32 = mybir.dt.float32
BF16 = mybir.dt.bfloat16
I32 = mybir.dt.int32
U32 = mybir.dt.uint32
U16 = mybir.dt.uint16
U8 = mybir.dt.uint8
FP8X4 = mybir.dt.float8_e4m3fn_x4
FP4X4 = mybir.dt.float4_e2m1fn_x4
ACT = mybir.ActivationFunctionType
ALU = mybir.AluOpType
AXIS = mybir.AxisListType

P = 128
PACK = 4
POOL = 2048
SLOTS = 512
HIDDEN = 512
TILES = HIDDEN // P
GROUPS = SLOTS // 8
RUN = 4
LINE = 2
VECTOR_TILES = 28
SCALAR_TILES = 21

FLOPS = 2 * 128 * 512 * 512 + 2 * 512 * 512 * 512 + 2 * 128 * 512 * 512


def tile_attend_lrshared_soft_kernel(tc, query, keys_words, keys_scales, tab_words, tab_scales, w1, temper, slot_factor, slot_scale, offs, out):
    nc = tc.nc
    with ExitStack() as ctx:
        keep = ctx.enter_context(tc.tile_pool(name="keep", bufs=1))
        psum = ctx.enter_context(tc.psum_pool(name="psum", bufs=8))

        def sbuf(name, shape, dtype, tag=None):
            return keep.tile(shape, dtype, name=name, tag=tag or name, align_bytes=64)

        def vector_tile(name, shape, dtype):
            return keep.tile(shape, dtype, name=name, tag="vector_out", bufs=VECTOR_TILES, align_bytes=64)

        def scalar_tile(name, shape, dtype):
            return keep.tile(shape, dtype, name=name, tag="scalar_out", bufs=SCALAR_TILES, align_bytes=64)

        def bank(name, shape):
            return psum.tile(shape, F32, name=name, tag="bank")

        def load_scale_rows(window, scales, queue):
            nc.vector.memset(window[:].bitcast(I32), 0)
            for quadrant in range(4):
                queue.dma_start(
                    out=window[32 * quadrant : 32 * quadrant + 4, :].bitcast(I32),
                    in_=scales[0, 4 * quadrant : 4 * quadrant + 4, :].bitcast(I32),
                )

        def gather(name, window, dtype):
            listed = vector_tile(name, [P, SLOTS], dtype)
            nc.vector.tensor_copy(listed[:], window[:].indirect(offsets[:]))
            return listed

        def round_and_weave(name, planes):
            woven = scalar_tile(name, [P, P, PACK], BF16)
            nc.scalar.copy(
                out=woven[:].rearrange("p (c i) t -> p c t i", i=RUN),
                in_=planes.rearrange("p t (c i) -> p c t i", i=RUN),
            )
            return woven

        def quantize(name, woven):
            codes = vector_tile(name + "_codes", [P, P], U32)
            scales = sbuf(name + "_scales", [P, P], U8)
            nc.vector.quantize_mx(out=codes[:].bitcast(FP8X4), scales=scales[:], in_=woven[:].rearrange("p c t -> p (c t)"))
            return codes, scales

        def product(result, stationary, moving, moving_dtype):
            nc.tensor.matmul_mx(
                out=result,
                lhsT=stationary[0][:].bitcast(FP8X4),
                lhsT_scale=stationary[1][:],
                rhs=moving[0][:].bitcast(moving_dtype),
                rhs_scale=moving[1][:],
                start=True,
                stop=True,
            )

        def turn_planes(name, planes):
            turned = bank(name, [P, PACK, P])
            for t in range(PACK):
                nc.tensor.transpose(turned[:, t, :], planes[:, t, :], identity[:])
            return turned

        tab_window = sbuf("tab_window", [P, POOL], U16)
        nc.sync.dma_start(out=tab_window[:].bitcast(I32), in_=tab_words[0].bitcast(I32))
        offsets = keep.tile([P, SLOTS // 16], U16, name="offsets")
        nc.sync.dma_start(offsets[:], offs)
        tab_scale_window = sbuf("tab_scale_window", [P, POOL], U8)
        load_scale_rows(tab_scale_window, tab_scales, nc.sync)

        def load_w1(first, count):
            raw = sbuf("w1_raw%d" % first, [P, PACK, P * count], F32)
            nc.sync.dma_start(out=raw[:], in_=w1[:, P * first : P * (first + count)].rearrange("(p t) r -> p t r", t=PACK))
            return [raw[:, :, P * j : P * (j + 1)] for j in range(count)]

        w1_raw = load_w1(0, 2)
        keys_window = sbuf("keys_window", [P, POOL], U16)
        nc.sync.dma_start(out=keys_window[:].bitcast(I32), in_=keys_words[0].bitcast(I32))
        query_raw = sbuf("query_raw", [P, PACK, P], F32)
        nc.sync.dma_start(out=query_raw[:], in_=query.rearrange("(p t) q -> p t q", t=PACK))
        keys_scale_window = sbuf("keys_scale_window", [P, POOL], U8)
        load_scale_rows(keys_scale_window, keys_scales, nc.sync)
        w1_raw.extend(load_w1(2, 2))

        temper_rows = sbuf("temper_rows", [P, P], F32)
        nc.gpsimd.memset(temper_rows[:], 0.0)
        nc.gpsimd.dma_start(out=temper_rows[0:TILES, :], in_=temper.rearrange("(j m) o -> j (m o)", m=P))
        identity = sbuf("identity", [P, P], F32)
        make_identity(nc, identity[:])
        vs_sb = sbuf("vs_sb", [P, PACK], F32)
        nc.gpsimd.dma_start(out=vs_sb[:], in_=slot_scale.rearrange("o (p t) -> (o p) t", t=PACK))
        os_sb = sbuf("os_sb", [P, PACK], F32)
        nc.gpsimd.dma_start(out=os_sb[:], in_=slot_factor.rearrange("o (p t) -> (o p) t", t=PACK))

        def w1_woven(j):
            return round_and_weave("w1_woven%d" % j, w1_raw[j])

        def listed_product(name, stationary, listed):
            sums = bank(name, [P, SLOTS])
            product(sums[:], stationary, listed, FP4X4)
            return sums

        def exponentials(j, zh):
            ht = scalar_tile("ht%d" % j, [P, PACK, P], F32)
            nc.scalar.activation(out=ht[:], in_=zh[:].rearrange("r (s t) -> r t s", t=PACK), func=ACT.Exp, scale=temper_sb[:, j : j + 1])
            return ht

        def group_sums(j, ht):
            sums = vector_tile("sums%d" % j, [P, GROUPS], F32)
            nc.vector.tensor_reduce(out=sums[:], in_=ht[:].rearrange("r t (g e) -> r g t e", e=2), axis=AXIS.XY, op=ALU.add)
            return sums

        def scaled_planes(j, turned):
            scaled = scalar_tile("scaled%d" % j, [P, PACK, P], F32)
            for t in range(PACK):
                nc.scalar.activation(out=scaled[:, t, :], in_=turned[:, t, :], func=ACT.Copy, scale=vs_sb[:, t : t + 1])
            return scaled

        def inverse_of(name, sums, width):
            inverse = vector_tile(name, [P, width], F32)
            nc.vector.reciprocal(inverse[:], sums[:])
            return inverse

        def doubled(j, inverse):
            twice = sbuf("doubled%d" % j, [P, GROUPS, 2], F32)
            nc.gpsimd.tensor_scalar(
                out=twice[:], in0=inverse[:].unsqueeze(2).to_broadcast([P, GROUPS, 2]), scalar1=4.0, scalar2=0.0, op0=ALU.mult, op1=ALU.add
            )
            return twice

        def turn_inverse(j, twice):
            turned = bank("inverse_turned%d" % j, [P, P])
            nc.tensor.transpose(turned[:], twice[:].rearrange("r g e -> r (g e)"), identity[:])
            return turned

        def values_woven(j, scaled, inverse):
            woven = vector_tile("values_woven%d" % j, [P, P, PACK], BF16)
            nc.vector.tensor_tensor(
                out=woven[:].rearrange("p (c i) t -> p c t i", i=LINE),
                in0=scaled[:].rearrange("p t (c i) -> p c t i", i=LINE),
                in1=inverse[:].rearrange("p (c i) -> p c i", i=LINE).unsqueeze(2).to_broadcast([P, P // LINE, PACK, LINE]),
                op=ALU.mult,
            )
            return woven

        def read_out(j, values, weights_mx):
            sums = bank("result%d" % j, [P, P])
            product(sums[:], weights_mx, values, FP8X4)
            result = scalar_tile("result_sb%d" % j, [P, P], F32)
            nc.scalar.copy(out=result[:], in_=sums[:])
            nc.sync.dma_start(out=out[:, P * j : P * (j + 1)], in_=result[:])

        def negated_max(scores):
            neg_max = vector_tile("neg_max", [P, 1], F32)
            nc.vector.tensor_reduce(out=neg_max[:], in_=scores[:], axis=AXIS.X, op=ALU.max, negate=True)
            return neg_max

        def softmax_terms(scores, neg_max):
            probs = scalar_tile("probs", [P, PACK, P], F32)
            row_sum = sbuf("row_sum", [P, 1], F32)
            nc.scalar.activation(
                out=probs[:], in_=scores[:].rearrange("q (s t) -> q t s", t=PACK), func=ACT.Exp, bias=neg_max[:], accum_out=row_sum[:]
            )
            return probs, row_sum

        def normalise(probs, row_inverse):
            normed = sbuf("normed", [P, PACK, P], F32)
            nc.gpsimd.tensor_scalar(out=normed[:], in0=probs[:], scalar1=row_inverse[:], scalar2=0.0, op0=ALU.mult, op1=ALU.add)
            return normed

        def weights_woven(turned):
            woven = vector_tile("weights_woven", [P, P, PACK], BF16)
            nc.vector.tensor_tensor(
                out=woven[:],
                in0=turned[:].rearrange("p t q -> p q t"),
                in1=os_sb[:].unsqueeze(1).to_broadcast([P, P, PACK]),
                op=ALU.mult,
            )
            return woven

        def factored_planes(turned):
            planes = scalar_tile("weights_planes", [P, PACK, P], BF16)
            for t in range(PACK):
                nc.scalar.activation(out=planes[:, t, :], in_=turned[:, t, :], func=ACT.Copy, scale=os_sb[:, t : t + 1])
            return planes

        def turn_temper():
            turned = bank("temper_turned", [P, P])
            nc.tensor.transpose(turned[:], temper_rows[:], identity[:])
            return turned

        def temper_columns(turned):
            columns = scalar_tile("temper_sb", [P, TILES], F32)
            nc.scalar.copy(out=columns[:], in_=turned[:, 0:TILES])
            return columns

        tab_listed = gather("tab_listed", tab_window, U16)
        tab_bytes = gather("tab_scales_listed", tab_scale_window, U8)
        w1_bf0 = w1_woven(0)
        w1_bf1 = w1_woven(1)
        temper_turned = turn_temper()
        temper_sb = temper_columns(temper_turned)
        w1_mx0 = quantize("w1_0", w1_bf0)
        zh0 = listed_product("zh0", w1_mx0, (tab_listed, tab_bytes))
        keys_listed = gather("keys_listed", keys_window, U16)
        query_bf = round_and_weave("query_woven", query_raw[:])
        w1_mx1 = quantize("w1_1", w1_bf1)
        zh1 = listed_product("zh1", w1_mx1, (tab_listed, tab_bytes))
        ht0 = exponentials(0, zh0)
        queries = quantize("query", query_bf)
        w1_bf2 = w1_woven(2)
        turned0 = turn_planes("ht_turned0", ht0)
        keys_bytes = gather("keys_scales_listed", keys_scale_window, U8)
        scores = listed_product("scores", queries, (keys_listed, keys_bytes))
        w1_bf3 = w1_woven(3)
        sums0 = group_sums(0, ht0)
        w1_mx2 = quantize("w1_2", w1_bf2)
        zh2 = listed_product("zh2", w1_mx2, (tab_listed, tab_bytes))
        ht1 = exponentials(1, zh1)
        w1_mx3 = quantize("w1_3", w1_bf3)
        zh3 = listed_product("zh3", w1_mx3, (tab_listed, tab_bytes))
        scaled0 = scaled_planes(0, turned0)
        inverse0 = inverse_of("inverse0", sums0, GROUPS)
        twice0 = doubled(0, inverse0)
        neg_max = negated_max(scores)
        turned1 = turn_planes("ht_turned1", ht1)
        ht2 = exponentials(2, zh2)
        probs, row_sum = softmax_terms(scores, neg_max)
        sums1 = group_sums(1, ht1)
        inverse_turned0 = turn_inverse(0, twice0)
        turned2 = turn_planes("ht_turned2", ht2)
        ht3 = exponentials(3, zh3)
        sums2 = group_sums(2, ht2)
        scaled1 = scaled_planes(1, turned1)
        row_inverse = inverse_of("row_inverse", row_sum, 1)
        normed = normalise(probs, row_inverse)
        inverse1 = inverse_of("inverse1", sums1, GROUPS)
        twice1 = doubled(1, inverse1)
        turned3 = turn_planes("ht_turned3", ht3)
        woven0 = values_woven(0, scaled0, inverse_turned0)
        scaled2 = scaled_planes(2, turned2)
        normed_turned = turn_planes("normed_turned", normed)
        inverse2 = inverse_of("inverse2", sums2, GROUPS)
        twice2 = doubled(2, inverse2)
        inverse_turned1 = turn_inverse(1, twice1)
        sums3 = group_sums(3, ht3)
        scaled3 = scaled_planes(3, turned3)
        values0 = quantize("values0", woven0)
        inverse_turned2 = turn_inverse(2, twice2)
        inverse3 = inverse_of("inverse3", sums3, GROUPS)
        twice3 = doubled(3, inverse3)
        weights_planes = factored_planes(normed_turned)
        woven1 = values_woven(1, scaled1, inverse_turned1)
        weights_bf = round_and_weave("weights_woven", weights_planes[:])
        inverse_turned3 = turn_inverse(3, twice3)
        woven2 = values_woven(2, scaled2, inverse_turned2)
        values1 = quantize("values1", woven1)
        weights_mx = quantize("weights", weights_bf)
        read_out(0, values0, weights_mx)
        read_out(1, values1, weights_mx)
        woven3 = values_woven(3, scaled3, inverse_turned3)
        values2 = quantize("values2", woven2)
        read_out(2, values2, weights_mx)
        values3 = quantize("values3", woven3)
        read_out(3, values3, weights_mx)
